import numpy as np
CORES = [4,12,20,28,36,44,52,60,132,140,148,156,164,172,180,188]
N = 16
H = 2
PERIODIC = True
def setup_inputs(rng):
    return {"x": rng.standard_normal((N, 128, 1024), dtype=np.float32)}
def reference(x):
    W = x.shape[2]
    y = np.zeros((N, 128, W + 2 * H), x.dtype)
    for r in range(N):
        y[r][:, H:H + W] = x[r]
        left, right = r - 1, r + 1
        if PERIODIC:
            left, right = left % N, right % N
        if 0 <= left < N:
            y[r][:, :H] = x[left][:, W - H:]
        if 0 <= right < N:
            y[r][:, W + H:] = x[right][:, :H]
    return {"y": y}

@@ -1,0 +1,59 @@
+from concourse.bass import DstId, RemoteDMATransfer
+
+H = 2
+
+SCRATCH = {
+    "edge": ("sbuf", [128, 2 * H], "float32"),
+    "halo": ("sbuf", [128, 2 * H], "float32"),
+}
+SEMAPHORES = ["loaded", "sent", "relay", "left", "right", "stored"]
+
+RIGHT_RELAY, LEFT_RELAY = 6, 2
+OFF_CHIP = 0x00FF
+
+
+def rank_program(g, core, T, topo):
+    n = len(T.cores)
+    sem = T.sem
+    rank = T.rank_of(core)
+
+    if rank is None:
+        local = core % 8
+        if local != RIGHT_RELAY and local != LEFT_RELAY:
+            return
+        owner = T.rank_of(core - local + 4)
+        if owner is None:
+            return
+        if local == RIGHT_RELAY:
+            dst, src_cols, dst_cols, arrive = T.cores[(owner + 1) % n], slice(H, 2 * H), slice(0, H), sem.left
+        else:
+            dst, src_cols, dst_cols, arrive = T.cores[(owner - 1) % n], slice(0, H), slice(H, 2 * H), sem.right
+        rid, pid = topo.addr(dst, core)
+        g.wait_ge(sem.relay, 8)
+        g.remote_dma(T.halo[:, dst_cols], T.edge[:, src_cols], arrive, sem.sent, pid, rid, OFF_CHIP)
+        g.wait_ge(sem.sent, 8)
+        return
+
+    W = T.x.shape[1]
+    g.sync.dma_start(T.edge[:, 0:H], T.x[:, 0:H]).then_inc(sem.loaded, 16)
+    g.scalar.dma_start(T.edge[:, H:2 * H], T.x[:, W - H:W]).then_inc(sem.loaded, 16)
+    g.sync.dma_start(T.y[:, H:H + W], T.x[:, :]).then_inc(sem.stored, 16)
+
+    base = core - core % 8
+    rr, rp = topo.addr(base + RIGHT_RELAY, core)
+    lr, lp = topo.addr(base + LEFT_RELAY, core)
+    g.wait_ge(sem.loaded, 32)
+    g.remote_dma_fused([
+        RemoteDMATransfer(dst_ids=[DstId(rid=rr, pnc=rp)], dma_engine_mask=0x00FF, remote_sem=sem.relay,
+                          src=T.edge[:, H:2 * H], dst=T.edge[:, H:2 * H]),
+        RemoteDMATransfer(dst_ids=[DstId(rid=lr, pnc=lp)], dma_engine_mask=0xFF00, remote_sem=sem.relay,
+                          src=T.edge[:, 0:H], dst=T.edge[:, 0:H]),
+    ], local_sem=sem.sent)
+
+    g.sync.wait_ge(sem.left, 8)
+    g.sync.dma_start(T.y[:, 0:H], T.halo[:, 0:H]).then_inc(sem.stored, 16)
+    g.scalar.wait_ge(sem.right, 8)
+    g.scalar.dma_start(T.y[:, H + W:2 * H + W], T.halo[:, H:2 * H]).then_inc(sem.stored, 16)
+
+    g.wait_ge(sem.sent, 16)
+    g.wait_ge(sem.stored, 48)

@@ -3,8 +3,8 @@ from concourse.bass import DstId, RemoteDMATransfer
 H = 2
 
 SCRATCH = {
-    "edge": ("sbuf", [128, 2 * H], "float32"),
-    "halo": ("sbuf", [128, 2 * H], "float32"),
+    "edge": ("dram", [2, 128, H], "float32"),
+    "halo": ("dram", [2, 128, H], "float32"),
 }
 SEMAPHORES = ["loaded", "sent", "relay", "left", "right", "stored"]
 
@@ -25,18 +25,18 @@ def rank_program(g, core, T, topo):
         if owner is None:
             return
         if local == RIGHT_RELAY:
-            dst, src_cols, dst_cols, arrive = T.cores[(owner + 1) % n], slice(H, 2 * H), slice(0, H), sem.left
+            dst, have, slot, arrive = T.cores[(owner + 1) % n], 1, 0, sem.left
         else:
-            dst, src_cols, dst_cols, arrive = T.cores[(owner - 1) % n], slice(0, H), slice(H, 2 * H), sem.right
+            dst, have, slot, arrive = T.cores[(owner - 1) % n], 0, 1, sem.right
         rid, pid = topo.addr(dst, core)
         g.wait_ge(sem.relay, 8)
-        g.remote_dma(T.halo[:, dst_cols], T.edge[:, src_cols], arrive, sem.sent, pid, rid, OFF_CHIP)
+        g.remote_dma(T.halo[slot], T.edge[have], arrive, sem.sent, pid, rid, OFF_CHIP)
         g.wait_ge(sem.sent, 8)
         return
 
     W = T.x.shape[1]
-    g.sync.dma_start(T.edge[:, 0:H], T.x[:, 0:H]).then_inc(sem.loaded, 16)
-    g.scalar.dma_start(T.edge[:, H:2 * H], T.x[:, W - H:W]).then_inc(sem.loaded, 16)
+    g.sync.dma_start(T.edge[0], T.x[:, 0:H]).then_inc(sem.loaded, 16)
+    g.scalar.dma_start(T.edge[1], T.x[:, W - H:W]).then_inc(sem.loaded, 16)
     g.sync.dma_start(T.y[:, H:H + W], T.x[:, :]).then_inc(sem.stored, 16)
 
     base = core - core % 8
@@ -45,15 +45,15 @@ def rank_program(g, core, T, topo):
     g.wait_ge(sem.loaded, 32)
     g.remote_dma_fused([
         RemoteDMATransfer(dst_ids=[DstId(rid=rr, pnc=rp)], dma_engine_mask=0x00FF, remote_sem=sem.relay,
-                          src=T.edge[:, H:2 * H], dst=T.edge[:, H:2 * H]),
+                          src=T.edge[1], dst=T.edge[1]),
         RemoteDMATransfer(dst_ids=[DstId(rid=lr, pnc=lp)], dma_engine_mask=0xFF00, remote_sem=sem.relay,
-                          src=T.edge[:, 0:H], dst=T.edge[:, 0:H]),
+                          src=T.edge[0], dst=T.edge[0]),
     ], local_sem=sem.sent)
 
     g.sync.wait_ge(sem.left, 8)
-    g.sync.dma_start(T.y[:, 0:H], T.halo[:, 0:H]).then_inc(sem.stored, 16)
+    g.sync.dma_start(T.y[:, 0:H], T.halo[0]).then_inc(sem.stored, 16)
     g.scalar.wait_ge(sem.right, 8)
-    g.scalar.dma_start(T.y[:, H + W:2 * H + W], T.halo[:, H:2 * H]).then_inc(sem.stored, 16)
+    g.scalar.dma_start(T.y[:, H + W:2 * H + W], T.halo[1]).then_inc(sem.stored, 16)
 
     g.wait_ge(sem.sent, 16)
     g.wait_ge(sem.stored, 48)

from concourse.bass import DstId, RemoteDMATransfer

H = 2

SCRATCH = {
    "edge": ("dram", [2, 128, H], "float32"),
    "halo": ("dram", [2, 128, H], "float32"),
}
SEMAPHORES = ["loaded", "sent", "relay", "left", "right", "stored"]

RIGHT_RELAY, LEFT_RELAY = 6, 2
OFF_CHIP = 0x00FF


def rank_program(g, core, T, topo):
    n = len(T.cores)
    sem = T.sem
    rank = T.rank_of(core)

    if rank is None:
        local = core % 8
        if local != RIGHT_RELAY and local != LEFT_RELAY:
            return
        owner = T.rank_of(core - local + 4)
        if owner is None:
            return
        if local == RIGHT_RELAY:
            dst, have, slot, arrive = T.cores[(owner + 1) % n], 1, 0, sem.left
        else:
            dst, have, slot, arrive = T.cores[(owner - 1) % n], 0, 1, sem.right
        rid, pid = topo.addr(dst, core)
        g.wait_ge(sem.relay, 8)
        g.remote_dma(T.halo[slot], T.edge[have], arrive, sem.sent, pid, rid, OFF_CHIP)
        g.wait_ge(sem.sent, 8)
        return

    W = T.x.shape[1]
    g.sync.dma_start(T.edge[0], T.x[:, 0:H]).then_inc(sem.loaded, 16)
    g.scalar.dma_start(T.edge[1], T.x[:, W - H:W]).then_inc(sem.loaded, 16)
    g.sync.dma_start(T.y[:, H:H + W], T.x[:, :]).then_inc(sem.stored, 16)

    base = core - core % 8
    rr, rp = topo.addr(base + RIGHT_RELAY, core)
    lr, lp = topo.addr(base + LEFT_RELAY, core)
    g.wait_ge(sem.loaded, 32)
    g.remote_dma_fused([
        RemoteDMATransfer(dst_ids=[DstId(rid=rr, pnc=rp)], dma_engine_mask=0x00FF, remote_sem=sem.relay,
                          src=T.edge[1], dst=T.edge[1]),
        RemoteDMATransfer(dst_ids=[DstId(rid=lr, pnc=lp)], dma_engine_mask=0xFF00, remote_sem=sem.relay,
                          src=T.edge[0], dst=T.edge[0]),
    ], local_sem=sem.sent)

    g.sync.wait_ge(sem.left, 8)
    g.sync.dma_start(T.y[:, 0:H], T.halo[0]).then_inc(sem.stored, 16)
    g.scalar.wait_ge(sem.right, 8)
    g.scalar.dma_start(T.y[:, H + W:2 * H + W], T.halo[1]).then_inc(sem.stored, 16)

    g.wait_ge(sem.sent, 16)
    g.wait_ge(sem.stored, 48)
